import numpy as np
import ml_dtypes


def mxq(x, axis, fmt="e4m3"):
    dtype, down = {"e4m3": (ml_dtypes.float8_e4m3fn, 7), "e5m2": (ml_dtypes.float8_e5m2, 14)}[fmt]
    v = np.moveaxis(np.asarray(x, np.float32).astype(ml_dtypes.bfloat16).astype(np.float64), axis, -1)
    blocks = v.reshape(v.shape[:-1] + (-1, 32))
    amax = np.abs(blocks).max(-1, keepdims=True)
    byte = np.maximum(np.where(amax > 0, np.frexp(amax)[1] - 1 + 127, 0) - down, 1)
    scale = np.exp2(byte - 127.0)
    codes = (blocks / scale).astype(np.float32).astype(dtype).astype(np.float64)
    return np.moveaxis((codes * scale).reshape(v.shape), -1, axis)


WIDE = False


def mx_kscale(k):
    if not WIDE:
        return np.ones(k)
    levels = np.array([10, -10, 5, -5, 0])
    if k % 512:
        return np.exp2(np.random.permutation(np.resize(levels, k // 32))).repeat(32)
    a = np.empty((k // 512, 16))
    for p in range(k // 512):
        a[p, :8] = np.random.permutation(np.resize(levels, 8))
        for g in range(8):
            far = levels[np.abs(levels - a[p, g]) >= 10]
            a[p, g + 8] = far[np.random.randint(len(far))]
    return np.exp2(a.ravel()).repeat(32)


def f64(x):
    return np.asarray(x).astype(np.float64)


def striped(idx):
    return np.tile(idx.reshape(-1, 16).T, (8, 1)).astype(np.uint16)


def unstriped(offs):
    return offs[:16].T.reshape(-1).astype(np.int64)


def silu(v):
    return v / (1.0 + np.exp(-np.maximum(v, -700.0)))


K, T, S, H, N = 1024, 1024, 512, 512, 256


def setup_inputs():
    n = np.random.standard_normal
    s = mx_kscale(K)[:, None]
    u = mx_kscale(H)
    return {
        "xT": (n((K, T)) * s).astype(np.float32),
        "w1": (n((K, H)) / np.sqrt(K) / s * u).astype(np.float32),
        "w2": (n((H, N)) / np.sqrt(H) / u[:, None]).astype(np.float32),
        "offs": striped(np.sort(np.random.permutation(T)[:S])),
    }


def reference(xT, w1, w2, offs):
    idx = unstriped(offs)
    xq = mxq(f64(xT)[:, idx], 0, "e4m3")
    h = silu(mxq(f64(w1), 0, "e4m3").T @ xq)
    y = mxq(f64(w2), 0, "e4m3").T @ mxq(h, 0, "e4m3")
    return y

@@ -1,0 +1,164 @@
+from contextlib import ExitStack
+
+import concourse.mybir as mybir
+from concourse.masks import make_identity
+
+K, T, S, H, N = 1024, 1024, 512, 512, 256
+FLOPS = 2 * S * (K * H + H * N)
+
+F32 = mybir.dt.float32
+BF16 = mybir.dt.bfloat16
+U32 = mybir.dt.uint32
+U16 = mybir.dt.uint16
+U8 = mybir.dt.uint8
+FP8X4 = mybir.dt.float8_e4m3fn_x4
+COPY = mybir.ActivationFunctionType.Copy
+SILU = mybir.ActivationFunctionType.Silu
+
+P = 128
+PASSES = K // 512
+G = 128
+GROUPS = S // G
+X_SCALAR = 896
+W_SCALAR = 32
+WARM = 24
+
+
+def tile_picked_pick_mlp_silu_srt_e_kernel(tc, xT, w1, w2, offs, out):
+    nc = tc.nc
+    with ExitStack() as ctx:
+        keep = ctx.enter_context(tc.tile_pool(name="keep", bufs=1))
+        psum = ctx.enter_context(tc.psum_pool(name="psum", bufs=1))
+
+        x_hbm = xT.rearrange("(s p j) t -> s p j t", p=P, j=4)
+        w1_hbm = w1.rearrange("(s p j) c -> s p j c", p=P, j=4)
+        w2_hbm = w2.rearrange("(p j) c -> p j c", j=4)
+        out_hbm = out.rearrange("(m p) n -> p m n", p=P)
+
+        offsets = keep.tile([P, S // 16], U16, name="offsets")
+        nc.sync.dma_start(offsets[:], offs)
+        x_raw = {}
+        for s in range(PASSES):
+            for u in range(2):
+                x_raw[s, u] = keep.tile([P, 2, T], F32, name="x_raw%d%d" % (s, u))
+                nc.sync.dma_start(x_raw[s, u][:], x_hbm[s, :, 2 * u : 2 * u + 2, :])
+        w1_raw = [keep.tile([P, 4, H], F32, name="w1_raw%d" % s) for s in range(PASSES)]
+        nc.sync.dma_start(w1_raw[0][:], w1_hbm[0])
+        for u in range(2):
+            nc.sync.dma_start(w1_raw[1][:, 2 * u : 2 * u + 2, :], w1_hbm[1, :, 2 * u : 2 * u + 2, :])
+        w2_raw = keep.tile([P, 4, N], F32, name="w2_raw")
+        nc.sync.dma_start(w2_raw[:], w2_hbm)
+
+        warm = keep.tile([P, 1], F32, name="warm")
+        nc.vector.memset(warm[:], 0.0)
+        nc.scalar.activation(warm[:], warm[:], SILU)
+
+        identity = keep.tile([P, P], BF16, name="identity")
+        make_identity(nc, identity[:])
+
+        x_codes, x_scales = [], []
+        for s in range(PASSES):
+            picked = keep.tile([P, S * 4], BF16, name="picked%d" % s, align_bytes=64)
+            picked_words = picked[:].bitcast(U32).rearrange("p (n u) -> p n u", u=2)
+            for u in range(2):
+                window = keep.tile([P, T * 2], BF16, name="window%d%d" % (s, u), align_bytes=64)
+                pairs = window[:].rearrange("p (t e) -> p t e", e=2)
+                raw = x_raw[s, u][:].rearrange("p e t -> p t e")
+                a = X_SCALAR
+                nc.scalar.activation(pairs[:, :a, :], raw[:, :a, :], COPY)
+                nc.vector.tensor_copy(pairs[:, a:, :], raw[:, a:, :])
+                nc.vector.tensor_copy(picked_words[:, :, u], window[:].bitcast(U32).indirect(offsets[:]))
+            codes = keep.tile([P, S], U32, name="x_codes%d" % s, align_bytes=64)
+            scales = keep.tile([P, S], U8, name="x_scales%d" % s, align_bytes=64)
+            nc.vector.quantize_mx(out=codes[:].bitcast(FP8X4), scales=scales[:], in_=picked[:])
+            x_codes.append(codes)
+            x_scales.append(scales)
+
+        w1_codes, w1_scales = [], []
+        for s in range(PASSES):
+            grouped = keep.tile([P, H * 4], BF16, name="w1_grouped%d" % s, align_bytes=64)
+            dst = grouped[:].rearrange("p (t m j) -> p m t j", t=4, j=4)
+            src = w1_raw[s][:].rearrange("p j (m t) -> p m t j", t=4)
+            a = W_SCALAR
+            for js in (range(0, 4),) if s == 0 else (range(0, 2), range(2, 4)):
+                lo, hi = js[0], js[-1] + 1
+                nc.scalar.activation(dst[:, :a, :, lo:hi], src[:, :a, :, lo:hi], COPY)
+                nc.vector.tensor_copy(dst[:, a:, :, lo:hi], src[:, a:, :, lo:hi])
+            codes = keep.tile([P, H], U32, name="w1_codes%d" % s, align_bytes=64)
+            scales = keep.tile([P, H], U8, name="w1_scales%d" % s, align_bytes=64)
+            width = H if s == 0 else 128
+            for c in range(0, H, width):
+                nc.vector.quantize_mx(
+                    out=codes[:, c : c + width].bitcast(FP8X4),
+                    scales=scales[:, c : c + width],
+                    in_=grouped[:, 4 * c : 4 * (c + width)],
+                )
+            if s == 0:
+                warm_bank = psum.tile([P, 4, P], BF16, name="warm_bank", tag="y_bank3")
+                for i in range(WARM):
+                    nc.tensor.transpose(warm_bank[:, i % 4, :], grouped[:, 128 * (i % 16) : 128 * (i % 16 + 1)], identity[:])
+            w1_codes.append(codes)
+            w1_scales.append(scales)
+
+        h_banks = [psum.tile([P, 4, G], F32, name="h_bank%d" % g) for g in range(GROUPS)]
+        y_banks = [psum.tile([P, 2, G], F32, name="y_bank%d" % g, tag="y_bank%d" % g) for g in range(GROUPS)]
+
+        def first_layer(g, t, s):
+            cols = slice(128 * t, 128 * (t + 1))
+            toks = slice(G * g, G * (g + 1))
+            nc.tensor.matmul_mx(
+                out=h_banks[g][:, t, :],
+                lhsT=w1_codes[s][:, cols].bitcast(FP8X4),
+                lhsT_scale=w1_scales[s][:, cols],
+                rhs=x_codes[s][:, toks].bitcast(FP8X4),
+                rhs_scale=x_scales[s][:, toks],
+                start=(s == 0),
+                stop=(s == PASSES - 1),
+            )
+
+        for g in range(GROUPS):
+            first_layer(g, 0, 0)
+
+        w2_grouped = keep.tile([P, N * 4], BF16, name="w2_grouped", align_bytes=64)
+        w2_codes = keep.tile([P, N], U32, name="w2_codes", align_bytes=64)
+        w2_scales = keep.tile([P, N], U8, name="w2_scales", align_bytes=64)
+
+        h_codes, h_scales = [], []
+        for g in range(GROUPS):
+            first_layer(g, 0, 1)
+            for t in range(1, 4):
+                for s in range(PASSES):
+                    first_layer(g, t, s)
+            hidden = keep.tile([P, G * 4], BF16, name="hidden%d" % g, align_bytes=64)
+            nc.scalar.activation(
+                hidden[:].rearrange("p (n t) -> p n t", t=4), h_banks[g][:].rearrange("p t n -> p n t"), SILU
+            )
+            codes = keep.tile([P, G], U32, name="h_codes%d" % g, align_bytes=64)
+            scales = keep.tile([P, G], U8, name="h_scales%d" % g, align_bytes=64)
+            nc.vector.quantize_mx(out=codes[:].bitcast(FP8X4), scales=scales[:], in_=hidden[:])
+            h_codes.append(codes)
+            h_scales.append(scales)
+            if g == 0:
+                nc.vector.tensor_copy(
+                    w2_grouped[:].rearrange("p (c j) -> p c j", j=4), w2_raw[:].rearrange("p j c -> p c j")
+                )
+                nc.vector.quantize_mx(out=w2_codes[:].bitcast(FP8X4), scales=w2_scales[:], in_=w2_grouped[:])
+
+        for g in range(GROUPS):
+            for m in range(2):
+                cols = slice(128 * m, 128 * (m + 1))
+                nc.tensor.matmul_mx(
+                    out=y_banks[g][:, m, :],
+                    lhsT=w2_codes[:, cols].bitcast(FP8X4),
+                    lhsT_scale=w2_scales[:, cols],
+                    rhs=h_codes[g][:].bitcast(FP8X4),
+                    rhs_scale=h_scales[g][:],
+                    start=True,
+                    stop=True,
+                )
+            result = keep.tile([P, 2, G], F32, name="result%d" % g)
+            if g == GROUPS - 1:
+                nc.scalar.activation(result[:], y_banks[g][:], COPY)
+            else:
+                nc.vector.tensor_copy(result[:], y_banks[g][:])
+            nc.sync.dma_start(out_hbm[:, :, G * g : G * (g + 1)], result[:])

@@ -19,9 +19,9 @@ P = 128
 PASSES = K // 512
 G = 128
 GROUPS = S // G
-X_SCALAR = 896
-W_SCALAR = 32
-WARM = 24
+X_SCALAR = ((256, 288), (704, 512))
+W1_SCALAR = (96, 56)
+WARM = 12
 
 
 def tile_picked_pick_mlp_silu_srt_e_kernel(tc, xT, w1, w2, offs, out):
@@ -30,135 +30,140 @@ def tile_picked_pick_mlp_silu_srt_e_kernel(tc, xT, w1, w2, offs, out):
         keep = ctx.enter_context(tc.tile_pool(name="keep", bufs=1))
         psum = ctx.enter_context(tc.psum_pool(name="psum", bufs=1))
 
-        x_hbm = xT.rearrange("(s p j) t -> s p j t", p=P, j=4)
+        x_hbm = xT.rearrange("(s p u e) t -> s u p e t", p=P, u=2, e=2)
         w1_hbm = w1.rearrange("(s p j) c -> s p j c", p=P, j=4)
         w2_hbm = w2.rearrange("(p j) c -> p j c", j=4)
         out_hbm = out.rearrange("(m p) n -> p m n", p=P)
 
         offsets = keep.tile([P, S // 16], U16, name="offsets")
-        nc.sync.dma_start(offsets[:], offs)
-        x_raw = {}
-        for s in range(PASSES):
-            for u in range(2):
-                x_raw[s, u] = keep.tile([P, 2, T], F32, name="x_raw%d%d" % (s, u))
-                nc.sync.dma_start(x_raw[s, u][:], x_hbm[s, :, 2 * u : 2 * u + 2, :])
+        x_raw = [[keep.tile([P, 2, T], F32, name="x_raw%d%d" % (s, u)) for u in range(2)] for s in range(PASSES)]
         w1_raw = [keep.tile([P, 4, H], F32, name="w1_raw%d" % s) for s in range(PASSES)]
-        nc.sync.dma_start(w1_raw[0][:], w1_hbm[0])
-        for u in range(2):
-            nc.sync.dma_start(w1_raw[1][:, 2 * u : 2 * u + 2, :], w1_hbm[1, :, 2 * u : 2 * u + 2, :])
         w2_raw = keep.tile([P, 4, N], F32, name="w2_raw")
+        nc.sync.dma_start(x_raw[0][0][:], x_hbm[0, 0])
+        nc.sync.dma_start(offsets[:], offs)
+        nc.sync.dma_start(x_raw[0][1][:], x_hbm[0, 1])
+        for u in range(2):
+            nc.sync.dma_start(x_raw[1][u][:], x_hbm[1, u])
+        for s in range(PASSES):
+            nc.sync.dma_start(w1_raw[s][:], w1_hbm[s])
         nc.sync.dma_start(w2_raw[:], w2_hbm)
 
-        warm = keep.tile([P, 1], F32, name="warm")
-        nc.vector.memset(warm[:], 0.0)
-        nc.scalar.activation(warm[:], warm[:], SILU)
-
+        table = keep.tile([P, 1], F32, name="table")
+        nc.vector.memset(table[:], 0.0)
+        nc.scalar.activation(table[:], table[:], SILU)
         identity = keep.tile([P, P], BF16, name="identity")
         make_identity(nc, identity[:])
 
-        x_codes, x_scales = [], []
+        def codes_and_scales(name, width):
+            codes = keep.tile([P, width], U32, name=name + "_codes", align_bytes=64)
+            scales = keep.tile([P, width], U8, name=name + "_scales", align_bytes=64)
+            return codes, scales
+
+        def quantize(pair, grouped, lo, hi):
+            codes, scales = pair
+            nc.vector.quantize_mx(
+                out=codes[:, lo:hi].bitcast(FP8X4), scales=scales[:, lo:hi], in_=grouped[:, 4 * lo : 4 * hi]
+            )
+
+        def matmul_mx(bank, stationary, cols, moving, toks, start, stop):
+            nc.tensor.matmul_mx(
+                out=bank,
+                lhsT=stationary[0][:, cols].bitcast(FP8X4),
+                lhsT_scale=stationary[1][:, cols],
+                rhs=moving[0][:, toks].bitcast(FP8X4),
+                rhs_scale=moving[1][:, toks],
+                start=start,
+                stop=stop,
+            )
+
+        warm_bank = psum.tile([P, 4, P], BF16, name="warm_bank", tag="y_bank2")
+        spare_bank = psum.tile([P, S], F32, name="spare_bank", tag="y_bank3")
+        h_banks = [psum.tile([P, 4, G], F32, name="h_bank%d" % g) for g in range(GROUPS)]
+
+        x_mx = []
         for s in range(PASSES):
-            picked = keep.tile([P, S * 4], BF16, name="picked%d" % s, align_bytes=64)
-            picked_words = picked[:].bitcast(U32).rearrange("p (n u) -> p n u", u=2)
+            planes = keep.tile([P, 2, S * 2], BF16, name="planes%d" % s, align_bytes=64)
             for u in range(2):
                 window = keep.tile([P, T * 2], BF16, name="window%d%d" % (s, u), align_bytes=64)
                 pairs = window[:].rearrange("p (t e) -> p t e", e=2)
-                raw = x_raw[s, u][:].rearrange("p e t -> p t e")
-                a = X_SCALAR
+                raw = x_raw[s][u][:].rearrange("p e t -> p t e")
+                a = X_SCALAR[s][u]
                 nc.scalar.activation(pairs[:, :a, :], raw[:, :a, :], COPY)
                 nc.vector.tensor_copy(pairs[:, a:, :], raw[:, a:, :])
-                nc.vector.tensor_copy(picked_words[:, :, u], window[:].bitcast(U32).indirect(offsets[:]))
-            codes = keep.tile([P, S], U32, name="x_codes%d" % s, align_bytes=64)
-            scales = keep.tile([P, S], U8, name="x_scales%d" % s, align_bytes=64)
-            nc.vector.quantize_mx(out=codes[:].bitcast(FP8X4), scales=scales[:], in_=picked[:])
-            x_codes.append(codes)
-            x_scales.append(scales)
+                nc.vector.tensor_copy(planes[:, u, :].bitcast(U32), window[:].bitcast(U32).indirect(offsets[:]))
+            picked = keep.tile([P, S * 4], BF16, name="picked%d" % s, align_bytes=64)
+            nc.vector.tensor_copy(
+                picked[:].rearrange("p (n u e) -> p n u e", u=2, e=2), planes[:].rearrange("p u (n e) -> p n u e", e=2)
+            )
+            x_mx.append(codes_and_scales("x%d" % s, S))
+            quantize(x_mx[s], picked, 0, S)
 
-        w1_codes, w1_scales = [], []
-        for s in range(PASSES):
-            grouped = keep.tile([P, H * 4], BF16, name="w1_grouped%d" % s, align_bytes=64)
-            dst = grouped[:].rearrange("p (t m j) -> p m t j", t=4, j=4)
-            src = w1_raw[s][:].rearrange("p j (m t) -> p m t j", t=4)
-            a = W_SCALAR
-            for js in (range(0, 4),) if s == 0 else (range(0, 2), range(2, 4)):
-                lo, hi = js[0], js[-1] + 1
-                nc.scalar.activation(dst[:, :a, :, lo:hi], src[:, :a, :, lo:hi], COPY)
-                nc.vector.tensor_copy(dst[:, a:, :, lo:hi], src[:, a:, :, lo:hi])
-            codes = keep.tile([P, H], U32, name="w1_codes%d" % s, align_bytes=64)
-            scales = keep.tile([P, H], U8, name="w1_scales%d" % s, align_bytes=64)
-            width = H if s == 0 else 128
-            for c in range(0, H, width):
-                nc.vector.quantize_mx(
-                    out=codes[:, c : c + width].bitcast(FP8X4),
-                    scales=scales[:, c : c + width],
-                    in_=grouped[:, 4 * c : 4 * (c + width)],
-                )
-            if s == 0:
-                warm_bank = psum.tile([P, 4, P], BF16, name="warm_bank", tag="y_bank3")
-                for i in range(WARM):
-                    nc.tensor.transpose(warm_bank[:, i % 4, :], grouped[:, 128 * (i % 16) : 128 * (i % 16 + 1)], identity[:])
-            w1_codes.append(codes)
-            w1_scales.append(scales)
+        for i in range(WARM):
+            nc.tensor.transpose(warm_bank[:, i % 4, :], picked[:, P * i : P * (i + 1)], identity[:])
 
-        h_banks = [psum.tile([P, 4, G], F32, name="h_bank%d" % g) for g in range(GROUPS)]
-        y_banks = [psum.tile([P, 2, G], F32, name="y_bank%d" % g, tag="y_bank%d" % g) for g in range(GROUPS)]
+        w1_mx = [codes_and_scales("w1_%d" % s, H) for s in range(PASSES)]
 
         def first_layer(g, t, s):
-            cols = slice(128 * t, 128 * (t + 1))
-            toks = slice(G * g, G * (g + 1))
-            nc.tensor.matmul_mx(
-                out=h_banks[g][:, t, :],
-                lhsT=w1_codes[s][:, cols].bitcast(FP8X4),
-                lhsT_scale=w1_scales[s][:, cols],
-                rhs=x_codes[s][:, toks].bitcast(FP8X4),
-                rhs_scale=x_scales[s][:, toks],
-                start=(s == 0),
-                stop=(s == PASSES - 1),
-            )
+            cols, toks = slice(P * t, P * (t + 1)), slice(G * g, G * (g + 1))
+            matmul_mx(h_banks[g][:, t, :], w1_mx[s], cols, x_mx[s], toks, s == 0, s == PASSES - 1)
 
-        for g in range(GROUPS):
-            first_layer(g, 0, 0)
+        for s in range(PASSES):
+            grouped = keep.tile([P, H * 4], BF16, name="w1_grouped%d" % s, align_bytes=64)
+            dst = grouped[:].rearrange("p (t m j) -> p m j t", t=4, j=4)
+            src = w1_raw[s][:].rearrange("p j (m t) -> p m j t", t=4)
+            a = W1_SCALAR[s]
+            nc.scalar.activation(dst[:, :a, :, :], src[:, :a, :, :], COPY)
+            nc.vector.tensor_copy(dst[:, a:, :, :], src[:, a:, :, :])
+            if s == 0:
+                quantize(w1_mx[s], grouped, 0, H)
+                matmul_mx(spare_bank[:], w1_mx[0], slice(0, P), x_mx[0], slice(0, S), True, True)
+                for g in range(GROUPS):
+                    first_layer(g, 0, 0)
+            else:
+                quantize(w1_mx[s], grouped, 0, H // 2)
+                quantize(w1_mx[s], grouped, H // 2, H)
 
+        y_banks = [psum.tile([P, 2, G], F32, name="y_bank%d" % g, tag="y_bank%d" % g) for g in range(GROUPS)]
+        hidden = [keep.tile([P, G * 4], BF16, name="hidden%d" % g, align_bytes=64) for g in range(GROUPS)]
+        h_mx = [codes_and_scales("h%d" % g, G) for g in range(GROUPS)]
+        results = [keep.tile([P, 2, G], F32, name="result%d" % g) for g in range(GROUPS)]
         w2_grouped = keep.tile([P, N * 4], BF16, name="w2_grouped", align_bytes=64)
-        w2_codes = keep.tile([P, N], U32, name="w2_codes", align_bytes=64)
-        w2_scales = keep.tile([P, N], U8, name="w2_scales", align_bytes=64)
+        w2_mx = codes_and_scales("w2", N)
 
-        h_codes, h_scales = [], []
-        for g in range(GROUPS):
+        def hide(g):
             first_layer(g, 0, 1)
             for t in range(1, 4):
                 for s in range(PASSES):
                     first_layer(g, t, s)
-            hidden = keep.tile([P, G * 4], BF16, name="hidden%d" % g, align_bytes=64)
             nc.scalar.activation(
-                hidden[:].rearrange("p (n t) -> p n t", t=4), h_banks[g][:].rearrange("p t n -> p n t"), SILU
+                hidden[g][:].rearrange("p (n t) -> p n t", t=4), h_banks[g][:].rearrange("p t n -> p n t"), SILU
             )
-            codes = keep.tile([P, G], U32, name="h_codes%d" % g, align_bytes=64)
-            scales = keep.tile([P, G], U8, name="h_scales%d" % g, align_bytes=64)
-            nc.vector.quantize_mx(out=codes[:].bitcast(FP8X4), scales=scales[:], in_=hidden[:])
-            h_codes.append(codes)
-            h_scales.append(scales)
-            if g == 0:
-                nc.vector.tensor_copy(
-                    w2_grouped[:].rearrange("p (c j) -> p c j", j=4), w2_raw[:].rearrange("p j c -> p c j")
-                )
-                nc.vector.quantize_mx(out=w2_codes[:].bitcast(FP8X4), scales=w2_scales[:], in_=w2_grouped[:])
 
-        for g in range(GROUPS):
+        def second_layer(g):
+            quantize(h_mx[g], hidden[g], 0, G)
             for m in range(2):
-                cols = slice(128 * m, 128 * (m + 1))
-                nc.tensor.matmul_mx(
-                    out=y_banks[g][:, m, :],
-                    lhsT=w2_codes[:, cols].bitcast(FP8X4),
-                    lhsT_scale=w2_scales[:, cols],
-                    rhs=h_codes[g][:].bitcast(FP8X4),
-                    rhs_scale=h_scales[g][:],
-                    start=True,
-                    stop=True,
-                )
-            result = keep.tile([P, 2, G], F32, name="result%d" % g)
-            if g == GROUPS - 1:
-                nc.scalar.activation(result[:], y_banks[g][:], COPY)
+                matmul_mx(y_banks[g][:, m, :], w2_mx, slice(P * m, P * (m + 1)), h_mx[g], slice(0, G), True, True)
+
+        def store(g):
+            if g == GROUPS - 2:
+                nc.scalar.activation(results[g][:], y_banks[g][:], COPY)
             else:
-                nc.vector.tensor_copy(result[:], y_banks[g][:])
-            nc.sync.dma_start(out_hbm[:, :, G * g : G * (g + 1)], result[:])
+                nc.vector.tensor_copy(results[g][:], y_banks[g][:])
+            nc.sync.dma_start(out_hbm[:, :, G * g : G * (g + 1)], results[g][:])
+
+        hide(0)
+        nc.vector.tensor_copy(
+            w2_grouped[:].rearrange("p (c i j) -> p c j i", i=4, j=4), w2_raw[:].rearrange("p j (c i) -> p c j i", i=4)
+        )
+        quantize(w2_mx, w2_grouped, 0, N)
+        hide(1)
+        hide(2)
+        second_layer(0)
+        hide(3)
+        second_layer(1)
+        store(0)
+        second_layer(2)
+        store(1)
+        second_layer(3)
+        store(2)
+        store(3)

from contextlib import ExitStack

import concourse.mybir as mybir
from concourse.masks import make_identity

K, T, S, H, N = 1024, 1024, 512, 512, 256
FLOPS = 2 * S * (K * H + H * N)

F32 = mybir.dt.float32
BF16 = mybir.dt.bfloat16
U32 = mybir.dt.uint32
U16 = mybir.dt.uint16
U8 = mybir.dt.uint8
FP8X4 = mybir.dt.float8_e4m3fn_x4
COPY = mybir.ActivationFunctionType.Copy
SILU = mybir.ActivationFunctionType.Silu

P = 128
PASSES = K // 512
G = 128
GROUPS = S // G
X_SCALAR = ((256, 288), (704, 512))
W1_SCALAR = (96, 56)
WARM = 12


def tile_picked_pick_mlp_silu_srt_e_kernel(tc, xT, w1, w2, offs, out):
    nc = tc.nc
    with ExitStack() as ctx:
        keep = ctx.enter_context(tc.tile_pool(name="keep", bufs=1))
        psum = ctx.enter_context(tc.psum_pool(name="psum", bufs=1))

        x_hbm = xT.rearrange("(s p u e) t -> s u p e t", p=P, u=2, e=2)
        w1_hbm = w1.rearrange("(s p j) c -> s p j c", p=P, j=4)
        w2_hbm = w2.rearrange("(p j) c -> p j c", j=4)
        out_hbm = out.rearrange("(m p) n -> p m n", p=P)

        offsets = keep.tile([P, S // 16], U16, name="offsets")
        x_raw = [[keep.tile([P, 2, T], F32, name="x_raw%d%d" % (s, u)) for u in range(2)] for s in range(PASSES)]
        w1_raw = [keep.tile([P, 4, H], F32, name="w1_raw%d" % s) for s in range(PASSES)]
        w2_raw = keep.tile([P, 4, N], F32, name="w2_raw")
        nc.sync.dma_start(x_raw[0][0][:], x_hbm[0, 0])
        nc.sync.dma_start(offsets[:], offs)
        nc.sync.dma_start(x_raw[0][1][:], x_hbm[0, 1])
        for u in range(2):
            nc.sync.dma_start(x_raw[1][u][:], x_hbm[1, u])
        for s in range(PASSES):
            nc.sync.dma_start(w1_raw[s][:], w1_hbm[s])
        nc.sync.dma_start(w2_raw[:], w2_hbm)

        table = keep.tile([P, 1], F32, name="table")
        nc.vector.memset(table[:], 0.0)
        nc.scalar.activation(table[:], table[:], SILU)
        identity = keep.tile([P, P], BF16, name="identity")
        make_identity(nc, identity[:])

        def codes_and_scales(name, width):
            codes = keep.tile([P, width], U32, name=name + "_codes", align_bytes=64)
            scales = keep.tile([P, width], U8, name=name + "_scales", align_bytes=64)
            return codes, scales

        def quantize(pair, grouped, lo, hi):
            codes, scales = pair
            nc.vector.quantize_mx(
                out=codes[:, lo:hi].bitcast(FP8X4), scales=scales[:, lo:hi], in_=grouped[:, 4 * lo : 4 * hi]
            )

        def matmul_mx(bank, stationary, cols, moving, toks, start, stop):
            nc.tensor.matmul_mx(
                out=bank,
                lhsT=stationary[0][:, cols].bitcast(FP8X4),
                lhsT_scale=stationary[1][:, cols],
                rhs=moving[0][:, toks].bitcast(FP8X4),
                rhs_scale=moving[1][:, toks],
                start=start,
                stop=stop,
            )

        warm_bank = psum.tile([P, 4, P], BF16, name="warm_bank", tag="y_bank2")
        spare_bank = psum.tile([P, S], F32, name="spare_bank", tag="y_bank3")
        h_banks = [psum.tile([P, 4, G], F32, name="h_bank%d" % g) for g in range(GROUPS)]

        x_mx = []
        for s in range(PASSES):
            planes = keep.tile([P, 2, S * 2], BF16, name="planes%d" % s, align_bytes=64)
            for u in range(2):
                window = keep.tile([P, T * 2], BF16, name="window%d%d" % (s, u), align_bytes=64)
                pairs = window[:].rearrange("p (t e) -> p t e", e=2)
                raw = x_raw[s][u][:].rearrange("p e t -> p t e")
                a = X_SCALAR[s][u]
                nc.scalar.activation(pairs[:, :a, :], raw[:, :a, :], COPY)
                nc.vector.tensor_copy(pairs[:, a:, :], raw[:, a:, :])
                nc.vector.tensor_copy(planes[:, u, :].bitcast(U32), window[:].bitcast(U32).indirect(offsets[:]))
            picked = keep.tile([P, S * 4], BF16, name="picked%d" % s, align_bytes=64)
            nc.vector.tensor_copy(
                picked[:].rearrange("p (n u e) -> p n u e", u=2, e=2), planes[:].rearrange("p u (n e) -> p n u e", e=2)
            )
            x_mx.append(codes_and_scales("x%d" % s, S))
            quantize(x_mx[s], picked, 0, S)

        for i in range(WARM):
            nc.tensor.transpose(warm_bank[:, i % 4, :], picked[:, P * i : P * (i + 1)], identity[:])

        w1_mx = [codes_and_scales("w1_%d" % s, H) for s in range(PASSES)]

        def first_layer(g, t, s):
            cols, toks = slice(P * t, P * (t + 1)), slice(G * g, G * (g + 1))
            matmul_mx(h_banks[g][:, t, :], w1_mx[s], cols, x_mx[s], toks, s == 0, s == PASSES - 1)

        for s in range(PASSES):
            grouped = keep.tile([P, H * 4], BF16, name="w1_grouped%d" % s, align_bytes=64)
            dst = grouped[:].rearrange("p (t m j) -> p m j t", t=4, j=4)
            src = w1_raw[s][:].rearrange("p j (m t) -> p m j t", t=4)
            a = W1_SCALAR[s]
            nc.scalar.activation(dst[:, :a, :, :], src[:, :a, :, :], COPY)
            nc.vector.tensor_copy(dst[:, a:, :, :], src[:, a:, :, :])
            if s == 0:
                quantize(w1_mx[s], grouped, 0, H)
                matmul_mx(spare_bank[:], w1_mx[0], slice(0, P), x_mx[0], slice(0, S), True, True)
                for g in range(GROUPS):
                    first_layer(g, 0, 0)
            else:
                quantize(w1_mx[s], grouped, 0, H // 2)
                quantize(w1_mx[s], grouped, H // 2, H)

        y_banks = [psum.tile([P, 2, G], F32, name="y_bank%d" % g, tag="y_bank%d" % g) for g in range(GROUPS)]
        hidden = [keep.tile([P, G * 4], BF16, name="hidden%d" % g, align_bytes=64) for g in range(GROUPS)]
        h_mx = [codes_and_scales("h%d" % g, G) for g in range(GROUPS)]
        results = [keep.tile([P, 2, G], F32, name="result%d" % g) for g in range(GROUPS)]
        w2_grouped = keep.tile([P, N * 4], BF16, name="w2_grouped", align_bytes=64)
        w2_mx = codes_and_scales("w2", N)

        def hide(g):
            first_layer(g, 0, 1)
            for t in range(1, 4):
                for s in range(PASSES):
                    first_layer(g, t, s)
            nc.scalar.activation(
                hidden[g][:].rearrange("p (n t) -> p n t", t=4), h_banks[g][:].rearrange("p t n -> p n t"), SILU
            )

        def second_layer(g):
            quantize(h_mx[g], hidden[g], 0, G)
            for m in range(2):
                matmul_mx(y_banks[g][:, m, :], w2_mx, slice(P * m, P * (m + 1)), h_mx[g], slice(0, G), True, True)

        def store(g):
            if g == GROUPS - 2:
                nc.scalar.activation(results[g][:], y_banks[g][:], COPY)
            else:
                nc.vector.tensor_copy(results[g][:], y_banks[g][:])
            nc.sync.dma_start(out_hbm[:, :, G * g : G * (g + 1)], results[g][:])

        hide(0)
        nc.vector.tensor_copy(
            w2_grouped[:].rearrange("p (c i j) -> p c j i", i=4, j=4), w2_raw[:].rearrange("p j (c i) -> p c j i", i=4)
        )
        quantize(w2_mx, w2_grouped, 0, N)
        hide(1)
        hide(2)
        second_layer(0)
        hide(3)
        second_layer(1)
        store(0)
        second_layer(2)
        store(1)
        second_layer(3)
        store(2)
        store(3)
